import numpy as np
CORES = [88,89,90,91,92,93,94,95,96,97,98,99,100,101,102,103]
N = 16
def setup_inputs(rng):
    return {"x1": rng.standard_normal((N, 128, 32), dtype=np.float32), "x2": rng.standard_normal((N, 128, 1), dtype=np.float32), "x3": rng.standard_normal((N, 128, 128), dtype=np.float32), "x4": rng.standard_normal((N, 128, 8), dtype=np.float32)}
def reference(x1, x2, x3, x4):
    out = {}
    s = x1.sum(axis=0, dtype=np.float64).astype(x1.dtype)
    out["y1"] = np.broadcast_to(s, (N,) + s.shape)
    s = x2.sum(axis=0, dtype=np.float64).astype(x2.dtype)
    out["y2"] = np.broadcast_to(s, (N,) + s.shape)
    s = x3.sum(axis=0, dtype=np.float64).astype(x3.dtype)
    out["y3"] = np.broadcast_to(s, (N,) + s.shape)
    s = x4.sum(axis=0, dtype=np.float64).astype(x4.dtype)
    out["y4"] = np.broadcast_to(s, (N,) + s.shape)
    return out

from concourse.bass import DstId, RemoteDMATransfer
from concourse.mybir import AluOpType

BLOCKS = [
    (2, 0, 32, [("1", 0, 128, 0, 128)]),
    (3, 1, 53, [("3", 23, 76, 0, 128)]),
    (6, 4, 32, [("4", 0, 128, 0, 32), ("2", 0, 128, 32, 36), ("3", 0, 23, 36, 128)]),
    (7, 5, 52, [("3", 76, 128, 0, 128)]),
]
NPIECES = sum(len(b[3]) for b in BLOCKS)

SCRATCH = {}
for bi, blk in enumerate(BLOCKS):
    SCRATCH["p%d" % bi] = ("dram", [128, blk[2]], "float32")
    SCRATCH["l%d" % bi] = ("dram", [8, 128, blk[2]], "float32")
    SCRATCH["pa%d" % bi] = ("dram", [128, blk[2]], "float32")
    SCRATCH["pb%d" % bi] = ("dram", [128, blk[2]], "float32")
    SCRATCH["r%d" % bi] = ("dram", [128, blk[2]], "float32")

SEMAPHORES = ["ld", "got", "part", "fin", "acc", "out", "sent"]

ON_CHIP = 0xFFFF
LOW8 = 0x00FF
HIGH8 = 0xFF00


def rank_program(g, core, T, topo):
    if T.rank_of(core) is None:
        return
    k = core % 8
    base = core - k
    far_base = [c - c % 8 for c in T.cores if c - c % 8 != base][0]
    S = T.sem
    queues = [g.sync, g.scalar]

    def did(c):
        a = topo.addr(c)
        return DstId(rid=a[0], pnc=a[1])

    n = 0
    for i, (col, fol, w, pieces) in enumerate(BLOCKS):
        for (t, a0, a1, b0, b1) in pieces:
            queues[n % 2].dma_start(T["p%d" % i][b0:b1, :], T["x" + t][a0:a1, :]).then_inc(S.ld, 16)
            n += 1
    g.wait_ge(S.ld, 16 * NPIECES)

    sent = 0
    for i, (col, fol, w, pieces) in enumerate(BLOCKS):
        if col == k:
            continue
        a = topo.addr(base + col)
        g.remote_dma(T["l%d" % i][k], T["p%d" % i][:], S.got, S.sent, a[1], a[0], ON_CHIP)
        sent += 16

    for i, (col, fol, w, pieces) in enumerate(BLOCKS):
        if k == col:
            g.wait_ge(S.got, 7 * 16)
            srcs = [T["p%d" % i][:] if j == k else T["l%d" % i][j] for j in range(8)]
            g.remote_dma_fused([
                RemoteDMATransfer(dst_ids=[did(far_base + fol)], dma_engine_mask=LOW8, remote_sem=S.part,
                                  srcs=srcs, dsts=[T["pb%d" % i][:]], alu_op=1),
                RemoteDMATransfer(dst_ids=[did(base + fol), did(base + fol)], dma_engine_mask=HIGH8, remote_sem=S.part,
                                  srcs=srcs, dsts=[T["pa%d" % i][:], T["r%d" % i][:]], alu_op=1),
            ], local_sem=S.sent)
            sent += 16
        if k == fol:
            g.wait_ge(S.part, 24)
            others = [base + c for c in range(8) if c != k]
            g.remote_dma_fused([
                RemoteDMATransfer(dst_ids=[did(c) for c in others], dma_engine_mask=ON_CHIP, remote_sem=S.fin,
                                  srcs=[T["pa%d" % i][:], T["pb%d" % i][:]],
                                  dsts=[T["r%d" % i][:] for c in others], alu_op=1),
            ], local_sem=S.sent)
            sent += 16
            g.dma_start(T["r%d" % i][:], T["pb%d" % i][:], accum_op=AluOpType.add,
                        max_dma_last_dim=8192).then_inc(S.acc, 16)
            g.wait_ge(S.acc, 16)
            g.sem_inc(S.fin, 16)

    for q in queues:
        q.wait_ge(S.fin, 64)
    n = 0
    for i, (col, fol, w, pieces) in enumerate(BLOCKS):
        for (t, a0, a1, b0, b1) in pieces:
            queues[n % 2].dma_start(T["y" + t][a0:a1, :], T["r%d" % i][b0:b1, :]).then_inc(S.out, 16)
            n += 1

    g.wait_ge(S.fin, 64)
    g.wait_ge(S.out, 16 * NPIECES)
    g.wait_ge(S.sent, sent)
